import numpy as np
import ml_dtypes


def mxq(x, axis, fmt="e4m3"):
    dtype, down = {"e4m3": (ml_dtypes.float8_e4m3fn, 7), "e5m2": (ml_dtypes.float8_e5m2, 14)}[fmt]
    v = np.moveaxis(np.asarray(x, np.float32).astype(ml_dtypes.bfloat16).astype(np.float64), axis, -1)
    blocks = v.reshape(v.shape[:-1] + (-1, 32))
    amax = np.abs(blocks).max(-1, keepdims=True)
    byte = np.maximum(np.where(amax > 0, np.frexp(amax)[1] - 1 + 127, 0) - down, 1)
    scale = np.exp2(byte - 127.0)
    codes = (blocks / scale).astype(np.float32).astype(dtype).astype(np.float64)
    return np.moveaxis((codes * scale).reshape(v.shape), -1, axis)


WIDE = False


def mx_kscale(k):
    if not WIDE:
        return np.ones(k)
    levels = np.array([30, -30])
    if k % 512:
        return np.exp2(np.random.permutation(np.resize(levels, k // 32))).repeat(32)
    a = np.empty((k // 512, 16))
    for p in range(k // 512):
        a[p, :8] = np.random.permutation(np.resize(levels, 8))
        for g in range(8):
            far = levels[np.abs(levels - a[p, g]) >= 10]
            a[p, g + 8] = far[np.random.randint(len(far))]
    return np.exp2(a.ravel()).repeat(32)


def f64(x):
    return np.asarray(x).astype(np.float64)


def striped(idx):
    return np.tile(np.asarray(idx).reshape(-1, 16).T, (8, 1)).astype(np.uint16)


def unstriped(offs):
    return offs[:16].T.reshape(-1).astype(np.int64)


E2M1 = np.array([0.0, 0.5, 1.0, 1.5, 2.0, 3.0, 4.0, 6.0, -0.0, -0.5, -1.0, -1.5, -2.0, -3.0, -4.0, -6.0])


def pack_weight(w, fmt):
    k, n = w.shape
    w = f64(np.asarray(w, np.float32).astype(ml_dtypes.bfloat16)).reshape(k // 32, 32, n)
    amax = np.abs(w).max(1)
    if fmt in ("e4m3", "e5m2"):
        byte = np.frexp(amax)[1] - 1 + 127 - (7 if fmt == "e4m3" else 14)
    else:
        mant, ex = np.frexp(amax / 6.0)
        byte = np.where(mant > 0.5, ex, ex - 1) + 127
    byte = np.clip(np.where(amax > 0, byte, 1), 1, 254)
    scaled = (w * np.exp2(127.0 - byte)[:, None, :]).reshape(k, n).astype(np.float32)
    by_word = np.ascontiguousarray(scaled.reshape(k // 512, 128, 4, n).transpose(0, 1, 3, 2))
    if fmt in ("e4m3", "e5m2"):
        words = by_word.astype(ml_dtypes.float8_e4m3fn if fmt == "e4m3" else ml_dtypes.float8_e5m2).view(np.uint8)
    else:
        c = by_word.astype(ml_dtypes.float4_e2m1fn).view(np.uint8) & 0xF
        words = (c[..., 0::2] | (c[..., 1::2] << 4)).reshape(k // 512, 128, 2 * n)
    return np.ascontiguousarray(words), np.ascontiguousarray(byte.astype(np.uint8).reshape(k // 512, 16, n))


def unpack_weight(words, scales, fmt):
    g, _, n = scales.shape
    words = np.ascontiguousarray(words).reshape(g, 128, n, -1)
    if fmt in ("e4m3", "e5m2"):
        vals = words.view(ml_dtypes.float8_e4m3fn if fmt == "e4m3" else ml_dtypes.float8_e5m2).astype(np.float64)
    else:
        nib = np.empty((g, 128, n, 4), np.uint8)
        nib[..., 0::2] = words & 0xF
        nib[..., 1::2] = words >> 4
        vals = E2M1[nib]
    vals = vals * np.repeat(np.exp2(scales.astype(np.float64) - 127.0), 8, axis=1)[..., None]
    return vals.transpose(0, 1, 3, 2).reshape(g * 512, n)


K, T, Z, J, R, C, O, N, L = 512, 1024, 1024, 256, 512, 512, 256, 256, 512


def setup_inputs():
    n = np.random.standard_normal
    idx = np.random.permutation(T)[:J]
    idx2 = np.random.permutation(Z)[:J]
    idx3 = np.random.permutation(C)[:J]
    idx4 = np.random.permutation(C)[:J]
    idx5 = np.random.permutation(C)[:O]
    idx6 = np.random.permutation(C)[:O]
    fk = mx_kscale(K)
    fr = mx_kscale(R)
    fl = mx_kscale(L)
    xtp = pack_weight(n((K, T)) / fk[:, None], "e4m3")
    xop = pack_weight(n((K, Z)) / fk[:, None], "e2m1")
    wp = pack_weight(n((K, R)) * 1 / np.sqrt(K) * fk[:, None] * fr, "e5m2")
    wbp = pack_weight(n((R, N)) * 1 / np.sqrt(R) / fr[:, None], "e5m2")
    sxp = pack_weight(n((L, O)) / fl[:, None], "e2m1")
    wsp = pack_weight(n((L, N)) * 1 / np.sqrt(L) * fl[:, None], "e5m2")
    return {
        "xt_words": xtp[0],
        "xt_scales": xtp[1],
        "xo_words": xop[0],
        "xo_scales": xop[1],
        "w_words": wp[0],
        "w_scales": wp[1],
        "wb_words": wbp[0],
        "wb_scales": wbp[1],
        "sx_words": sxp[0],
        "sx_scales": sxp[1],
        "ws_words": wsp[0],
        "ws_scales": wsp[1],
        "offs": striped(idx),
        "offs2": striped(idx2),
        "offs3": striped(idx3),
        "offs4": striped(idx4),
        "offs5": striped(idx5),
        "offs6": striped(idx6),
    }


def reference(xt_words, xt_scales, xo_words, xo_scales, w_words, w_scales, wb_words, wb_scales, sx_words, sx_scales, ws_words, ws_scales, offs, offs2, offs3, offs4, offs5, offs6):
    idx = unstriped(offs)
    idx2 = unstriped(offs2)
    idx3 = unstriped(offs3)
    idx4 = unstriped(offs4)
    idx5 = unstriped(offs5)
    idx6 = unstriped(offs6)
    xtu = unpack_weight(xt_words, xt_scales, "e4m3")
    xou = unpack_weight(xo_words, xo_scales, "e2m1")
    wu = unpack_weight(w_words, w_scales, "e5m2")
    wbu = unpack_weight(wb_words, wb_scales, "e5m2")
    sxu = unpack_weight(sx_words, sx_scales, "e2m1")
    wsu = unpack_weight(ws_words, ws_scales, "e5m2")
    xtidxg = xtu[:, idx]
    a = wu.T @ xtidxg
    xoidx2g = xou[:, idx2]
    b = wu.T @ xoidx2g
    pw = np.zeros((R, C))
    pw[:, idx3] = a
    pv = np.zeros((R, C))
    pv[:, idx4] = b
    hid = np.maximum(pw[:, idx5], pv[:, idx6])
    hidq = mxq(hid, 0, "e4m3")
    y = wbu.T @ hidq + wsu.T @ sxu
    return y

@@ -1,0 +1,176 @@
+from contextlib import ExitStack
+
+import concourse.mybir as mybir
+
+K, T, Z, J, R, C, O, N, L = 512, 1024, 1024, 256, 512, 512, 256, 256, 512
+FLOPS = 2 * K * R * J * 2 + 2 * R * N * O + 2 * L * N * O
+
+F32 = mybir.dt.float32
+BF16 = mybir.dt.bfloat16
+I32 = mybir.dt.int32
+U32 = mybir.dt.uint32
+U16 = mybir.dt.uint16
+U8 = mybir.dt.uint8
+E4M3 = mybir.dt.float8_e4m3fn_x4
+E5M2 = mybir.dt.float8_e5m2_x4
+E2M1 = mybir.dt.float4_e2m1fn_x4
+COPY = mybir.ActivationFunctionType.Copy
+MAX = mybir.AluOpType.max
+
+P = 128
+PACK = 4
+HALF = O // 2
+
+
+def tile_list_oneforboth_twoboards_skip_plain_kernel(tc, xt_words, xt_scales, xo_words, xo_scales, w_words, w_scales, wb_words, wb_scales,
+        sx_words, sx_scales, ws_words, ws_scales, offs, offs2, offs3, offs4, offs5, offs6, out):
+    nc = tc.nc
+
+    with ExitStack() as ctx:
+        lists = ctx.enter_context(tc.tile_pool(name="lists", bufs=1))
+        sb = ctx.enter_context(tc.tile_pool(name="sb", bufs=1))
+        ps = ctx.enter_context(tc.psum_pool(name="ps", bufs=1))
+
+        def load_list(src, name):
+            tile = lists.tile([P, J // 16], U16, name=name)
+            nc.sync.dma_start(tile[:], src)
+            return tile
+
+        def load_words(queue, src, width, dtype, name):
+            tile = sb.tile([P, width], dtype, name=name, align_bytes=64)
+            queue.dma_start(tile[:].bitcast(I32), src.bitcast(I32))
+            return tile
+
+        def load_scale_rows(queue, plane, src, q):
+            queue.dma_start(plane[32 * q : 32 * q + 4, :].bitcast(I32), src[0][4 * q : 4 * q + 4, :].bitcast(I32))
+
+        def fp8_rows(words):
+            return words[0].rearrange("p n t -> p (n t)")
+
+        def move(engine, dst, src):
+            if engine == "vector":
+                nc.vector.tensor_copy(dst, src)
+            else:
+                nc.scalar.activation(dst, src, COPY)
+
+        xo_s = sb.tile([P, Z], U8, name="xo_s", align_bytes=64)
+        xt_s = sb.tile([P, T], U8, name="xt_s", tag="xt_s", align_bytes=64)
+        wt_s = sb.tile([P, R + 3 * N], U8, name="wt_s", align_bytes=64)
+        for plane in (xo_s, wt_s, xt_s):
+            nc.vector.memset(plane[:].bitcast(I32), 0)
+        w_s = wt_s[:, 0:R]
+        wb_s = wt_s[:, R : R + N]
+        ws_s = wt_s[:, R + N : R + 2 * N]
+        sx_s = wt_s[:, R + 2 * N : R + 3 * N]
+
+        l2 = load_list(offs2, "l2")
+        xo_w = load_words(nc.sync, xo_words[0], Z, U16, "xo_w")
+        w_w = load_words(nc.scalar, fp8_rows(w_words), R, U32, "w_w")
+        load_scale_rows(nc.sync, xo_s, xo_scales, 0)
+        load_scale_rows(nc.scalar, xo_s, xo_scales, 1)
+        load_scale_rows(nc.sync, xo_s, xo_scales, 2)
+        load_scale_rows(nc.scalar, xo_s, xo_scales, 3)
+        load_scale_rows(nc.scalar, w_s, w_scales, 0)
+        for q in range(1, 4):
+            load_scale_rows(nc.sync, w_s, w_scales, q)
+        l4 = load_list(offs4, "l4")
+        l1 = load_list(offs, "l1")
+        xt_w = load_words(nc.sync, fp8_rows(xt_words), T, U32, "xt_w")
+        for q in range(4):
+            load_scale_rows(nc.sync, xt_s, xt_scales, q)
+        l3 = load_list(offs3, "l3")
+        l6 = load_list(offs6, "l6")
+        l5 = load_list(offs5, "l5")
+        ws_w = load_words(nc.sync, fp8_rows(ws_words), N, U32, "ws_w")
+        sx_w = load_words(nc.sync, sx_words[0], O, U16, "sx_w")
+        for q in range(4):
+            load_scale_rows(nc.sync, ws_s, ws_scales, q)
+            load_scale_rows(nc.sync, sx_s, sx_scales, q)
+        wb_w = load_words(nc.sync, fp8_rows(wb_words), N, U32, "wb_w")
+        for q in range(4):
+            load_scale_rows(nc.sync, wb_s, wb_scales, q)
+
+        pv = [sb.tile([P, C], F32, name=f"pv{t}") for t in range(PACK)]
+        pw = [sb.tile([P, C], F32, name=f"pw{t}") for t in range(PACK)]
+        for board in pv + pw:
+            nc.vector.memset(board[:], 0.0)
+
+        xo_gw = sb.tile([P, J], U16, name="xo_gw", align_bytes=64)
+        xo_gs = sb.tile([P, J], U8, name="xo_gs", align_bytes=64)
+        xt_gw = sb.tile([P, J], U32, name="xt_gw", align_bytes=64)
+        xt_gs = sb.tile([P, J], U8, name="xt_gs", align_bytes=64)
+        wp_w = sb.tile([P, R], U32, name="wp_w", align_bytes=64)
+        wp_s = sb.tile([P, R], U8, name="wp_s", align_bytes=64)
+
+        nc.vector.tensor_copy(xo_gw[:], xo_w[:].indirect(l2[:]))
+        nc.vector.tensor_copy(
+            wp_w[:].rearrange("p (t c i) -> p c t i", t=PACK, i=4),
+            w_w[:].rearrange("p (c i t) -> p c t i", t=PACK, i=4),
+        )
+        nc.vector.tensor_copy(xo_gs[:], xo_s[:].indirect(l2[:]))
+        nc.vector.tensor_copy(
+            wp_s[:].rearrange("p (t c i) -> p c t i", t=PACK, i=16),
+            w_s.rearrange("p (c i t) -> p c t i", t=PACK, i=16),
+        )
+
+        def product(t, words, scales, tag):
+            bank = ps.tile([P, J], F32, name=tag, tag=tag)
+            cols = slice(t * P, (t + 1) * P)
+            nc.tensor.matmul_mx(bank[:], wp_w[:, cols].bitcast(E5M2), wp_s[:, cols], words, scales, start=True, stop=True)
+            return bank
+
+        def place(engine, bank, board, places, tag):
+            stage = sb.tile([P, J], F32, name=tag, tag=tag, align_bytes=64)
+            move(engine, stage[:], bank[:])
+            move(engine, board[:].indirect(places[:]), stage[:])
+
+        b_banks = [product(t, xo_gw[:].bitcast(E2M1), xo_gs[:], f"b{t}") for t in range(PACK)]
+        nc.vector.tensor_copy(xt_gw[:], xt_w[:].indirect(l1[:]))
+        place("scalar", b_banks[0], pv[0], l4, "sb0")
+        place("vector", b_banks[1], pv[1], l4, "sb1")
+        place("scalar", b_banks[2], pv[2], l4, "sb2")
+        nc.vector.tensor_copy(xt_gs[:], xt_s[:].indirect(l1[:]))
+        a_banks = [product(t, xt_gw[:].bitcast(E4M3), xt_gs[:], f"a{t}") for t in range(PACK)]
+        place("vector", b_banks[3], pv[3], l4, "xt_s")
+        place("scalar", a_banks[0], pw[0], l3, "sa0")
+        place("vector", a_banks[1], pw[1], l3, "sa1")
+        place("scalar", a_banks[2], pw[2], l3, "sa2")
+        place("vector", a_banks[3], pw[3], l3, "sa3")
+
+        y_banks = []
+        for h in range(2):
+            bank = ps.tile([P, 2, HALF], F32, name=f"y{h}", tag=f"b{h}")
+            cols = slice(h * HALF, (h + 1) * HALF)
+            for nh in range(2):
+                ncols = slice(nh * P, (nh + 1) * P)
+                nc.tensor.matmul_mx(bank[:, nh, :], ws_w[:, ncols].bitcast(E5M2), ws_s[:, ncols],
+                                    sx_w[:, cols].bitcast(E2M1), sx_s[:, cols], start=(nh == 0), stop=False)
+            y_banks.append(bank)
+
+        vector_picks = [{("v", 3), ("w", 1), ("w", 3)}, {("w", 1), ("w", 3)}]
+        out_v = out.rearrange("(g p) o -> p g o", p=P)
+        for h in range(2):
+            entries = slice(h * HALF // 16, (h + 1) * HALF // 16)
+            gv = sb.tile([P, PACK, HALF], F32, name=f"gv{h}")
+            gw = sb.tile([P, PACK, HALF], F32, name=f"gw{h}")
+            for kind, boards, picks, dst in (("v", pv, l6, gv), ("w", pw, l5, gw)):
+                for t in range(PACK):
+                    engine = "vector" if (kind, t) in vector_picks[h] else "scalar"
+                    move(engine, dst[:, t, :], boards[t][:].indirect(picks[:, entries]))
+            hid = sb.tile([P, HALF * PACK], BF16, name=f"hid{h}", align_bytes=64)
+            nc.vector.tensor_tensor(
+                hid[:].rearrange("p (c i t) -> p c t i", t=PACK, i=4),
+                gw[:].rearrange("p t (c i) -> p c t i", i=4),
+                gv[:].rearrange("p t (c i) -> p c t i", i=4),
+                MAX,
+            )
+            hid_w = sb.tile([P, HALF], U32, name=f"hid_w{h}", align_bytes=64)
+            hid_s = sb.tile([P, HALF], U8, name=f"hid_s{h}", align_bytes=64)
+            nc.vector.quantize_mx(hid_w[:].bitcast(E4M3), hid_s[:], hid[:])
+            for nh in range(2):
+                ncols = slice(nh * P, (nh + 1) * P)
+                nc.tensor.matmul_mx(y_banks[h][:, nh, :], wb_w[:, ncols].bitcast(E5M2), wb_s[:, ncols],
+                                    hid_w[:].bitcast(E4M3), hid_s[:], start=False, stop=(nh == 1))
+            y = sb.tile([P, 2, HALF], F32, name=f"y_sb{h}")
+            move("scalar", y[:], y_banks[h][:])
+            nc.sync.dma_start(out_v[:, :, h * HALF : (h + 1) * HALF], y[:])

@@ -36,8 +36,8 @@ def tile_list_oneforboth_twoboards_skip_plain_kernel(tc, xt_words, xt_scales, xo
             nc.sync.dma_start(tile[:], src)
             return tile
 
-        def load_words(queue, src, width, dtype, name):
-            tile = sb.tile([P, width], dtype, name=name, align_bytes=64)
+        def load_words(queue, src, width, dtype, name, tag=""):
+            tile = sb.tile([P, width], dtype, name=name, tag=tag or name, align_bytes=64)
             queue.dma_start(tile[:].bitcast(I32), src.bitcast(I32))
             return tile
 
@@ -55,52 +55,41 @@ def tile_list_oneforboth_twoboards_skip_plain_kernel(tc, xt_words, xt_scales, xo
 
         xo_s = sb.tile([P, Z], U8, name="xo_s", align_bytes=64)
         xt_s = sb.tile([P, T], U8, name="xt_s", tag="xt_s", align_bytes=64)
-        wt_s = sb.tile([P, R + 3 * N], U8, name="wt_s", align_bytes=64)
-        for plane in (xo_s, wt_s, xt_s):
-            nc.vector.memset(plane[:].bitcast(I32), 0)
-        w_s = wt_s[:, 0:R]
-        wb_s = wt_s[:, R : R + N]
-        ws_s = wt_s[:, R + N : R + 2 * N]
-        sx_s = wt_s[:, R + 2 * N : R + 3 * N]
+        w_st = sb.tile([P, R], U8, name="w_s", align_bytes=64)
+        nc.vector.memset(xo_s[:].bitcast(I32), 0)
+        nc.vector.memset(w_st[:].bitcast(I32), 0)
+        nc.vector.memset(xt_s[:].bitcast(I32), 0)
+        w_s = w_st[:, :]
 
         l2 = load_list(offs2, "l2")
         xo_w = load_words(nc.sync, xo_words[0], Z, U16, "xo_w")
-        w_w = load_words(nc.scalar, fp8_rows(w_words), R, U32, "w_w")
-        load_scale_rows(nc.sync, xo_s, xo_scales, 0)
-        load_scale_rows(nc.scalar, xo_s, xo_scales, 1)
-        load_scale_rows(nc.sync, xo_s, xo_scales, 2)
-        load_scale_rows(nc.scalar, xo_s, xo_scales, 3)
-        load_scale_rows(nc.scalar, w_s, w_scales, 0)
-        for q in range(1, 4):
-            load_scale_rows(nc.sync, w_s, w_scales, q)
-        l4 = load_list(offs4, "l4")
-        l1 = load_list(offs, "l1")
-        xt_w = load_words(nc.sync, fp8_rows(xt_words), T, U32, "xt_w")
         for q in range(4):
-            load_scale_rows(nc.sync, xt_s, xt_scales, q)
+            load_scale_rows(nc.sync if q == 1 else nc.scalar, xo_s, xo_scales, q)
+        w_w = load_words(nc.sync, fp8_rows(w_words), R, U32, "w_w")
+        for q in range(4):
+            load_scale_rows(nc.sync if q else nc.scalar, w_s, w_scales, q)
+        xt_w = load_words(nc.sync, fp8_rows(xt_words), T, U32, "xt_w")
+        l1 = load_list(offs, "l1")
+        l4 = load_list(offs4, "l4")
+        for q in range(4):
+            load_scale_rows(nc.gpsimd if q < 2 else nc.sync, xt_s, xt_scales, q)
         l3 = load_list(offs3, "l3")
         l6 = load_list(offs6, "l6")
         l5 = load_list(offs5, "l5")
-        ws_w = load_words(nc.sync, fp8_rows(ws_words), N, U32, "ws_w")
-        sx_w = load_words(nc.sync, sx_words[0], O, U16, "sx_w")
-        for q in range(4):
-            load_scale_rows(nc.sync, ws_s, ws_scales, q)
-            load_scale_rows(nc.sync, sx_s, sx_scales, q)
-        wb_w = load_words(nc.sync, fp8_rows(wb_words), N, U32, "wb_w")
-        for q in range(4):
-            load_scale_rows(nc.sync, wb_s, wb_scales, q)
 
-        pv = [sb.tile([P, C], F32, name=f"pv{t}") for t in range(PACK)]
-        pw = [sb.tile([P, C], F32, name=f"pw{t}") for t in range(PACK)]
-        for board in pv + pw:
-            nc.vector.memset(board[:], 0.0)
+        def board(name, tag, engine):
+            tile = sb.tile([P, C], F32, name=name, tag=tag, align_bytes=64)
+            engine.memset(tile[:], 0.0)
+            return tile
+
+        pv = [board("pv0", "pv0", nc.vector), board("pv1", "pv1", nc.vector)]
 
         xo_gw = sb.tile([P, J], U16, name="xo_gw", align_bytes=64)
         xo_gs = sb.tile([P, J], U8, name="xo_gs", align_bytes=64)
         xt_gw = sb.tile([P, J], U32, name="xt_gw", align_bytes=64)
         xt_gs = sb.tile([P, J], U8, name="xt_gs", align_bytes=64)
         wp_w = sb.tile([P, R], U32, name="wp_w", align_bytes=64)
-        wp_s = sb.tile([P, R], U8, name="wp_s", align_bytes=64)
+        wp_s = [sb.tile([P, P], U8, name=f"wp_s{t}", align_bytes=64) for t in range(PACK)]
 
         nc.vector.tensor_copy(xo_gw[:], xo_w[:].indirect(l2[:]))
         nc.vector.tensor_copy(
@@ -108,63 +97,81 @@ def tile_list_oneforboth_twoboards_skip_plain_kernel(tc, xt_words, xt_scales, xo
             w_w[:].rearrange("p (c i t) -> p c t i", t=PACK, i=4),
         )
         nc.vector.tensor_copy(xo_gs[:], xo_s[:].indirect(l2[:]))
-        nc.vector.tensor_copy(
-            wp_s[:].rearrange("p (t c i) -> p c t i", t=PACK, i=16),
-            w_s.rearrange("p (c i t) -> p c t i", t=PACK, i=16),
-        )
+        for t in range(PACK):
+            nc.vector.tensor_copy(wp_s[t][:], w_s[:, t::PACK])
+        pv.append(board("pv2", "w_s", nc.gpsimd))
 
         def product(t, words, scales, tag):
             bank = ps.tile([P, J], F32, name=tag, tag=tag)
             cols = slice(t * P, (t + 1) * P)
-            nc.tensor.matmul_mx(bank[:], wp_w[:, cols].bitcast(E5M2), wp_s[:, cols], words, scales, start=True, stop=True)
+            nc.tensor.matmul_mx(bank[:], wp_w[:, cols].bitcast(E5M2), wp_s[t][:], words, scales, start=True, stop=True)
             return bank
 
-        def place(engine, bank, board, places, tag):
-            stage = sb.tile([P, J], F32, name=tag, tag=tag, align_bytes=64)
-            move(engine, stage[:], bank[:])
-            move(engine, board[:].indirect(places[:]), stage[:])
+        def place(engine, banks, boards, places, tag):
+            stage = sb.tile([P, 2 * J], F32, name=tag, tag=tag, align_bytes=64)
+            for i, bank in enumerate(banks):
+                move(engine, stage[:, i * J : (i + 1) * J], bank[:])
+            for i, board in enumerate(boards):
+                move(engine, board[:].indirect(places[:]), stage[:, i * J : (i + 1) * J])
 
         b_banks = [product(t, xo_gw[:].bitcast(E2M1), xo_gs[:], f"b{t}") for t in range(PACK)]
+        place("scalar", b_banks[0:2], pv[0:2], l4, "sb01")
         nc.vector.tensor_copy(xt_gw[:], xt_w[:].indirect(l1[:]))
-        place("scalar", b_banks[0], pv[0], l4, "sb0")
-        place("vector", b_banks[1], pv[1], l4, "sb1")
-        place("scalar", b_banks[2], pv[2], l4, "sb2")
+        pv.append(board("pv3", "xt_w", nc.gpsimd))
         nc.vector.tensor_copy(xt_gs[:], xt_s[:].indirect(l1[:]))
+        pw = [board("pw0", "xo_gw", nc.gpsimd), board("pw1", "xo_gs", nc.gpsimd)]
         a_banks = [product(t, xt_gw[:].bitcast(E4M3), xt_gs[:], f"a{t}") for t in range(PACK)]
-        place("vector", b_banks[3], pv[3], l4, "xt_s")
-        place("scalar", a_banks[0], pw[0], l3, "sa0")
-        place("vector", a_banks[1], pw[1], l3, "sa1")
-        place("scalar", a_banks[2], pw[2], l3, "sa2")
-        place("vector", a_banks[3], pw[3], l3, "sa3")
+        pw = pw + [board("pw2", "wp_s0", nc.gpsimd), board("pw3", "wp_s1", nc.gpsimd)]
+        place("vector", b_banks[2:4], pv[2:4], l4, "xt_s")
+        place("scalar", a_banks[0:2], pw[0:2], l3, "sa01")
+        place("vector", a_banks[2:4], pw[2:4], l3, "sa23")
 
-        y_banks = []
+        late_s = sb.tile([P, 3 * N], U8, name="late_s", tag="wp_s2", align_bytes=64)
+        nc.gpsimd.memset(late_s[:].bitcast(I32), 0)
+        wb_s = late_s[:, 0:N]
+        ws_s = late_s[:, N : 2 * N]
+        sx_s = late_s[:, 2 * N : 3 * N]
+        ws_w = load_words(nc.sync, fp8_rows(ws_words), N, U32, "ws_w", "xo_w")
+        sx_w = load_words(nc.sync, sx_words[0], O, U16, "sx_w", "xt_gs")
+        for q in range(4):
+            load_scale_rows(nc.sync, ws_s, ws_scales, q)
+            load_scale_rows(nc.sync, sx_s, sx_scales, q)
+        wb_w = load_words(nc.sync, fp8_rows(wb_words), N, U32, "wb_w", "xt_gw")
+        for q in range(4):
+            load_scale_rows(nc.sync, wb_s, wb_scales, q)
+
+        y_banks = [ps.tile([P, 2, HALF], F32, name=f"y{h}", tag=f"b{h}") for h in range(2)]
         for h in range(2):
-            bank = ps.tile([P, 2, HALF], F32, name=f"y{h}", tag=f"b{h}")
             cols = slice(h * HALF, (h + 1) * HALF)
             for nh in range(2):
                 ncols = slice(nh * P, (nh + 1) * P)
-                nc.tensor.matmul_mx(bank[:, nh, :], ws_w[:, ncols].bitcast(E5M2), ws_s[:, ncols],
+                nc.tensor.matmul_mx(y_banks[h][:, nh, :], ws_w[:, ncols].bitcast(E5M2), ws_s[:, ncols],
                                     sx_w[:, cols].bitcast(E2M1), sx_s[:, cols], start=(nh == 0), stop=False)
-            y_banks.append(bank)
 
-        vector_picks = [{("v", 3), ("w", 1), ("w", 3)}, {("w", 1), ("w", 3)}]
+        vector_picks = [{("v", 3), ("w", 2), ("w", 3)}, {("w", 2), ("w", 3)}]
         out_v = out.rearrange("(g p) o -> p g o", p=P)
-        for h in range(2):
+        gv = [sb.tile([P, PACK, HALF], F32, name=f"gv{h}") for h in range(2)]
+        gw = [sb.tile([P, PACK, HALF], F32, name=f"gw{h}", align_bytes=64) for h in range(2)]
+
+        def pick(h):
             entries = slice(h * HALF // 16, (h + 1) * HALF // 16)
-            gv = sb.tile([P, PACK, HALF], F32, name=f"gv{h}")
-            gw = sb.tile([P, PACK, HALF], F32, name=f"gw{h}")
-            for kind, boards, picks, dst in (("v", pv, l6, gv), ("w", pw, l5, gw)):
+            for kind, boards, picks, dst in (("v", pv, l6, gv[h]), ("w", pw, l5, gw[h])):
                 for t in range(PACK):
                     engine = "vector" if (kind, t) in vector_picks[h] else "scalar"
                     move(engine, dst[:, t, :], boards[t][:].indirect(picks[:, entries]))
+
+        def larger(h):
             hid = sb.tile([P, HALF * PACK], BF16, name=f"hid{h}", align_bytes=64)
             nc.vector.tensor_tensor(
                 hid[:].rearrange("p (c i t) -> p c t i", t=PACK, i=4),
-                gw[:].rearrange("p t (c i) -> p c t i", i=4),
-                gv[:].rearrange("p t (c i) -> p c t i", i=4),
+                gw[h][:].rearrange("p t (c i) -> p c t i", i=4),
+                gv[h][:].rearrange("p t (c i) -> p c t i", i=4),
                 MAX,
             )
-            hid_w = sb.tile([P, HALF], U32, name=f"hid_w{h}", align_bytes=64)
+            return hid
+
+        def finish(h, hid, tag, engine, queue):
+            hid_w = sb.tile([P, HALF], U32, name=f"hid_w{h}", tag=tag, align_bytes=64)
             hid_s = sb.tile([P, HALF], U8, name=f"hid_s{h}", align_bytes=64)
             nc.vector.quantize_mx(hid_w[:].bitcast(E4M3), hid_s[:], hid[:])
             for nh in range(2):
@@ -172,5 +179,12 @@ def tile_list_oneforboth_twoboards_skip_plain_kernel(tc, xt_words, xt_scales, xo
                 nc.tensor.matmul_mx(y_banks[h][:, nh, :], wb_w[:, ncols].bitcast(E5M2), wb_s[:, ncols],
                                     hid_w[:].bitcast(E4M3), hid_s[:], start=False, stop=(nh == 1))
             y = sb.tile([P, 2, HALF], F32, name=f"y_sb{h}")
-            move("scalar", y[:], y_banks[h][:])
-            nc.sync.dma_start(out_v[:, :, h * HALF : (h + 1) * HALF], y[:])
+            move(engine, y[:], y_banks[h][:])
+            queue.dma_start(out_v[:, :, h * HALF : (h + 1) * HALF], y[:])
+
+        hids = []
+        for h in range(2):
+            pick(h)
+            hids.append(larger(h))
+        finish(0, hids[0], "gw1", "scalar", nc.scalar)
+        finish(1, hids[1], "hid_w1", "vector", nc.sync)

@@ -60,6 +60,11 @@ def tile_list_oneforboth_twoboards_skip_plain_kernel(tc, xt_words, xt_scales, xo
         nc.vector.memset(w_st[:].bitcast(I32), 0)
         nc.vector.memset(xt_s[:].bitcast(I32), 0)
         w_s = w_st[:, :]
+        late_s = sb.tile([P, 3 * N], U8, name="late_s", align_bytes=64)
+        nc.vector.memset(late_s[:].bitcast(I32), 0)
+        wb_s = late_s[:, 0:N]
+        ws_s = late_s[:, N : 2 * N]
+        sx_s = late_s[:, 2 * N : 3 * N]
 
         l2 = load_list(offs2, "l2")
         xo_w = load_words(nc.sync, xo_words[0], Z, U16, "xo_w")
@@ -72,17 +77,23 @@ def tile_list_oneforboth_twoboards_skip_plain_kernel(tc, xt_words, xt_scales, xo
         l1 = load_list(offs, "l1")
         l4 = load_list(offs4, "l4")
         for q in range(4):
-            load_scale_rows(nc.gpsimd if q < 2 else nc.sync, xt_s, xt_scales, q)
+            load_scale_rows(nc.sync, xt_s, xt_scales, q)
         l3 = load_list(offs3, "l3")
         l6 = load_list(offs6, "l6")
         l5 = load_list(offs5, "l5")
+        ws_w = load_words(nc.sync, fp8_rows(ws_words), N, U32, "ws_w")
+        sx_w = load_words(nc.sync, sx_words[0], O, U16, "sx_w")
+        for q in range(4):
+            load_scale_rows(nc.sync, ws_s, ws_scales, q)
+            load_scale_rows(nc.sync, sx_s, sx_scales, q)
+        wb_w = load_words(nc.sync, fp8_rows(wb_words), N, U32, "wb_w")
+        for q in range(4):
+            load_scale_rows(nc.sync, wb_s, wb_scales, q)
 
-        def board(name, tag, engine):
-            tile = sb.tile([P, C], F32, name=name, tag=tag, align_bytes=64)
-            engine.memset(tile[:], 0.0)
-            return tile
-
-        pv = [board("pv0", "pv0", nc.vector), board("pv1", "pv1", nc.vector)]
+        pv = [sb.tile([P, C], F32, name=f"pv{t}") for t in range(PACK)]
+        pw = [sb.tile([P, C], F32, name=f"pw{t}") for t in range(PACK)]
+        for board in pv + pw:
+            nc.vector.memset(board[:], 0.0)
 
         xo_gw = sb.tile([P, J], U16, name="xo_gw", align_bytes=64)
         xo_gs = sb.tile([P, J], U8, name="xo_gs", align_bytes=64)
@@ -99,7 +110,6 @@ def tile_list_oneforboth_twoboards_skip_plain_kernel(tc, xt_words, xt_scales, xo
         nc.vector.tensor_copy(xo_gs[:], xo_s[:].indirect(l2[:]))
         for t in range(PACK):
             nc.vector.tensor_copy(wp_s[t][:], w_s[:, t::PACK])
-        pv.append(board("pv2", "w_s", nc.gpsimd))
 
         def product(t, words, scales, tag):
             bank = ps.tile([P, J], F32, name=tag, tag=tag)
@@ -117,28 +127,11 @@ def tile_list_oneforboth_twoboards_skip_plain_kernel(tc, xt_words, xt_scales, xo
         b_banks = [product(t, xo_gw[:].bitcast(E2M1), xo_gs[:], f"b{t}") for t in range(PACK)]
         place("scalar", b_banks[0:2], pv[0:2], l4, "sb01")
         nc.vector.tensor_copy(xt_gw[:], xt_w[:].indirect(l1[:]))
-        pv.append(board("pv3", "xt_w", nc.gpsimd))
         nc.vector.tensor_copy(xt_gs[:], xt_s[:].indirect(l1[:]))
-        pw = [board("pw0", "xo_gw", nc.gpsimd), board("pw1", "xo_gs", nc.gpsimd)]
         a_banks = [product(t, xt_gw[:].bitcast(E4M3), xt_gs[:], f"a{t}") for t in range(PACK)]
-        pw = pw + [board("pw2", "wp_s0", nc.gpsimd), board("pw3", "wp_s1", nc.gpsimd)]
         place("vector", b_banks[2:4], pv[2:4], l4, "xt_s")
         place("scalar", a_banks[0:2], pw[0:2], l3, "sa01")
         place("vector", a_banks[2:4], pw[2:4], l3, "sa23")
-
-        late_s = sb.tile([P, 3 * N], U8, name="late_s", tag="wp_s2", align_bytes=64)
-        nc.gpsimd.memset(late_s[:].bitcast(I32), 0)
-        wb_s = late_s[:, 0:N]
-        ws_s = late_s[:, N : 2 * N]
-        sx_s = late_s[:, 2 * N : 3 * N]
-        ws_w = load_words(nc.sync, fp8_rows(ws_words), N, U32, "ws_w", "xo_w")
-        sx_w = load_words(nc.sync, sx_words[0], O, U16, "sx_w", "xt_gs")
-        for q in range(4):
-            load_scale_rows(nc.sync, ws_s, ws_scales, q)
-            load_scale_rows(nc.sync, sx_s, sx_scales, q)
-        wb_w = load_words(nc.sync, fp8_rows(wb_words), N, U32, "wb_w", "xt_gw")
-        for q in range(4):
-            load_scale_rows(nc.sync, wb_s, wb_scales, q)
 
         y_banks = [ps.tile([P, 2, HALF], F32, name=f"y{h}", tag=f"b{h}") for h in range(2)]
         for h in range(2):
@@ -163,9 +156,9 @@ def tile_list_oneforboth_twoboards_skip_plain_kernel(tc, xt_words, xt_scales, xo
         def larger(h):
             hid = sb.tile([P, HALF * PACK], BF16, name=f"hid{h}", align_bytes=64)
             nc.vector.tensor_tensor(
-                hid[:].rearrange("p (c i t) -> p c t i", t=PACK, i=4),
-                gw[h][:].rearrange("p t (c i) -> p c t i", i=4),
-                gv[h][:].rearrange("p t (c i) -> p c t i", i=4),
+                hid[:].rearrange("p (c i t) -> p c t i", t=PACK, i=2),
+                gw[h][:].rearrange("p t (c i) -> p c t i", i=2),
+                gv[h][:].rearrange("p t (c i) -> p c t i", i=2),
                 MAX,
             )
             return hid

from contextlib import ExitStack

import concourse.mybir as mybir

K, T, Z, J, R, C, O, N, L = 512, 1024, 1024, 256, 512, 512, 256, 256, 512
FLOPS = 2 * K * R * J * 2 + 2 * R * N * O + 2 * L * N * O

F32 = mybir.dt.float32
BF16 = mybir.dt.bfloat16
I32 = mybir.dt.int32
U32 = mybir.dt.uint32
U16 = mybir.dt.uint16
U8 = mybir.dt.uint8
E4M3 = mybir.dt.float8_e4m3fn_x4
E5M2 = mybir.dt.float8_e5m2_x4
E2M1 = mybir.dt.float4_e2m1fn_x4
COPY = mybir.ActivationFunctionType.Copy
MAX = mybir.AluOpType.max

P = 128
PACK = 4
HALF = O // 2


def tile_list_oneforboth_twoboards_skip_plain_kernel(tc, xt_words, xt_scales, xo_words, xo_scales, w_words, w_scales, wb_words, wb_scales,
        sx_words, sx_scales, ws_words, ws_scales, offs, offs2, offs3, offs4, offs5, offs6, out):
    nc = tc.nc

    with ExitStack() as ctx:
        lists = ctx.enter_context(tc.tile_pool(name="lists", bufs=1))
        sb = ctx.enter_context(tc.tile_pool(name="sb", bufs=1))
        ps = ctx.enter_context(tc.psum_pool(name="ps", bufs=1))

        def load_list(src, name):
            tile = lists.tile([P, J // 16], U16, name=name)
            nc.sync.dma_start(tile[:], src)
            return tile

        def load_words(queue, src, width, dtype, name, tag=""):
            tile = sb.tile([P, width], dtype, name=name, tag=tag or name, align_bytes=64)
            queue.dma_start(tile[:].bitcast(I32), src.bitcast(I32))
            return tile

        def load_scale_rows(queue, plane, src, q):
            queue.dma_start(plane[32 * q : 32 * q + 4, :].bitcast(I32), src[0][4 * q : 4 * q + 4, :].bitcast(I32))

        def fp8_rows(words):
            return words[0].rearrange("p n t -> p (n t)")

        def move(engine, dst, src):
            if engine == "vector":
                nc.vector.tensor_copy(dst, src)
            else:
                nc.scalar.activation(dst, src, COPY)

        xo_s = sb.tile([P, Z], U8, name="xo_s", align_bytes=64)
        xt_s = sb.tile([P, T], U8, name="xt_s", tag="xt_s", align_bytes=64)
        w_st = sb.tile([P, R], U8, name="w_s", align_bytes=64)
        nc.vector.memset(xo_s[:].bitcast(I32), 0)
        nc.vector.memset(w_st[:].bitcast(I32), 0)
        nc.vector.memset(xt_s[:].bitcast(I32), 0)
        w_s = w_st[:, :]
        late_s = sb.tile([P, 3 * N], U8, name="late_s", align_bytes=64)
        nc.vector.memset(late_s[:].bitcast(I32), 0)
        wb_s = late_s[:, 0:N]
        ws_s = late_s[:, N : 2 * N]
        sx_s = late_s[:, 2 * N : 3 * N]

        l2 = load_list(offs2, "l2")
        xo_w = load_words(nc.sync, xo_words[0], Z, U16, "xo_w")
        for q in range(4):
            load_scale_rows(nc.sync if q == 1 else nc.scalar, xo_s, xo_scales, q)
        w_w = load_words(nc.sync, fp8_rows(w_words), R, U32, "w_w")
        for q in range(4):
            load_scale_rows(nc.sync if q else nc.scalar, w_s, w_scales, q)
        xt_w = load_words(nc.sync, fp8_rows(xt_words), T, U32, "xt_w")
        l1 = load_list(offs, "l1")
        l4 = load_list(offs4, "l4")
        for q in range(4):
            load_scale_rows(nc.sync, xt_s, xt_scales, q)
        l3 = load_list(offs3, "l3")
        l6 = load_list(offs6, "l6")
        l5 = load_list(offs5, "l5")
        ws_w = load_words(nc.sync, fp8_rows(ws_words), N, U32, "ws_w")
        sx_w = load_words(nc.sync, sx_words[0], O, U16, "sx_w")
        for q in range(4):
            load_scale_rows(nc.sync, ws_s, ws_scales, q)
            load_scale_rows(nc.sync, sx_s, sx_scales, q)
        wb_w = load_words(nc.sync, fp8_rows(wb_words), N, U32, "wb_w")
        for q in range(4):
            load_scale_rows(nc.sync, wb_s, wb_scales, q)

        pv = [sb.tile([P, C], F32, name=f"pv{t}") for t in range(PACK)]
        pw = [sb.tile([P, C], F32, name=f"pw{t}") for t in range(PACK)]
        for board in pv + pw:
            nc.vector.memset(board[:], 0.0)

        xo_gw = sb.tile([P, J], U16, name="xo_gw", align_bytes=64)
        xo_gs = sb.tile([P, J], U8, name="xo_gs", align_bytes=64)
        xt_gw = sb.tile([P, J], U32, name="xt_gw", align_bytes=64)
        xt_gs = sb.tile([P, J], U8, name="xt_gs", align_bytes=64)
        wp_w = sb.tile([P, R], U32, name="wp_w", align_bytes=64)
        wp_s = [sb.tile([P, P], U8, name=f"wp_s{t}", align_bytes=64) for t in range(PACK)]

        nc.vector.tensor_copy(xo_gw[:], xo_w[:].indirect(l2[:]))
        nc.vector.tensor_copy(
            wp_w[:].rearrange("p (t c i) -> p c t i", t=PACK, i=4),
            w_w[:].rearrange("p (c i t) -> p c t i", t=PACK, i=4),
        )
        nc.vector.tensor_copy(xo_gs[:], xo_s[:].indirect(l2[:]))
        for t in range(PACK):
            nc.vector.tensor_copy(wp_s[t][:], w_s[:, t::PACK])

        def product(t, words, scales, tag):
            bank = ps.tile([P, J], F32, name=tag, tag=tag)
            cols = slice(t * P, (t + 1) * P)
            nc.tensor.matmul_mx(bank[:], wp_w[:, cols].bitcast(E5M2), wp_s[t][:], words, scales, start=True, stop=True)
            return bank

        def place(engine, banks, boards, places, tag):
            stage = sb.tile([P, 2 * J], F32, name=tag, tag=tag, align_bytes=64)
            for i, bank in enumerate(banks):
                move(engine, stage[:, i * J : (i + 1) * J], bank[:])
            for i, board in enumerate(boards):
                move(engine, board[:].indirect(places[:]), stage[:, i * J : (i + 1) * J])

        b_banks = [product(t, xo_gw[:].bitcast(E2M1), xo_gs[:], f"b{t}") for t in range(PACK)]
        place("scalar", b_banks[0:2], pv[0:2], l4, "sb01")
        nc.vector.tensor_copy(xt_gw[:], xt_w[:].indirect(l1[:]))
        nc.vector.tensor_copy(xt_gs[:], xt_s[:].indirect(l1[:]))
        a_banks = [product(t, xt_gw[:].bitcast(E4M3), xt_gs[:], f"a{t}") for t in range(PACK)]
        place("vector", b_banks[2:4], pv[2:4], l4, "xt_s")
        place("scalar", a_banks[0:2], pw[0:2], l3, "sa01")
        place("vector", a_banks[2:4], pw[2:4], l3, "sa23")

        y_banks = [ps.tile([P, 2, HALF], F32, name=f"y{h}", tag=f"b{h}") for h in range(2)]
        for h in range(2):
            cols = slice(h * HALF, (h + 1) * HALF)
            for nh in range(2):
                ncols = slice(nh * P, (nh + 1) * P)
                nc.tensor.matmul_mx(y_banks[h][:, nh, :], ws_w[:, ncols].bitcast(E5M2), ws_s[:, ncols],
                                    sx_w[:, cols].bitcast(E2M1), sx_s[:, cols], start=(nh == 0), stop=False)

        vector_picks = [{("v", 3), ("w", 2), ("w", 3)}, {("w", 2), ("w", 3)}]
        out_v = out.rearrange("(g p) o -> p g o", p=P)
        gv = [sb.tile([P, PACK, HALF], F32, name=f"gv{h}") for h in range(2)]
        gw = [sb.tile([P, PACK, HALF], F32, name=f"gw{h}", align_bytes=64) for h in range(2)]

        def pick(h):
            entries = slice(h * HALF // 16, (h + 1) * HALF // 16)
            for kind, boards, picks, dst in (("v", pv, l6, gv[h]), ("w", pw, l5, gw[h])):
                for t in range(PACK):
                    engine = "vector" if (kind, t) in vector_picks[h] else "scalar"
                    move(engine, dst[:, t, :], boards[t][:].indirect(picks[:, entries]))

        def larger(h):
            hid = sb.tile([P, HALF * PACK], BF16, name=f"hid{h}", align_bytes=64)
            nc.vector.tensor_tensor(
                hid[:].rearrange("p (c i t) -> p c t i", t=PACK, i=2),
                gw[h][:].rearrange("p t (c i) -> p c t i", i=2),
                gv[h][:].rearrange("p t (c i) -> p c t i", i=2),
                MAX,
            )
            return hid

        def finish(h, hid, tag, engine, queue):
            hid_w = sb.tile([P, HALF], U32, name=f"hid_w{h}", tag=tag, align_bytes=64)
            hid_s = sb.tile([P, HALF], U8, name=f"hid_s{h}", align_bytes=64)
            nc.vector.quantize_mx(hid_w[:].bitcast(E4M3), hid_s[:], hid[:])
            for nh in range(2):
                ncols = slice(nh * P, (nh + 1) * P)
                nc.tensor.matmul_mx(y_banks[h][:, nh, :], wb_w[:, ncols].bitcast(E5M2), wb_s[:, ncols],
                                    hid_w[:].bitcast(E4M3), hid_s[:], start=False, stop=(nh == 1))
            y = sb.tile([P, 2, HALF], F32, name=f"y_sb{h}")
            move(engine, y[:], y_banks[h][:])
            queue.dma_start(out_v[:, :, h * HALF : (h + 1) * HALF], y[:])

        hids = []
        for h in range(2):
            pick(h)
            hids.append(larger(h))
        finish(0, hids[0], "gw1", "scalar", nc.scalar)
        finish(1, hids[1], "hid_w1", "vector", nc.sync)
